import numpy as np
import ml_dtypes

BF16 = ml_dtypes.bfloat16


def bf(x):
    return np.asarray(x, np.float32).astype(BF16)


def f32(x):
    return np.asarray(x, np.float32)


def f64(x):
    return np.asarray(x).astype(np.float64)


def striped(idx):
    return np.tile(idx.reshape(-1, 16).T, (8, 1))


S, A, K, M, N, E, Q = 512, 128, 256, 512, 128, 1, 128


def gelu_tanh(v):
    return 0.5 * v * (1.0 + np.tanh(np.sqrt(2.0 / np.pi) * (v + 0.044715 * v**3)))


def setup_inputs():
    return {"x": bf(np.random.standard_normal((A, S))), "wd": bf(np.random.standard_normal((A, M)) / np.sqrt(A)), "y": bf(np.random.standard_normal((K, N))), "w": bf(np.random.standard_normal((K, M)) / np.sqrt(K)), "b": f32(0.5 * np.random.standard_normal((M, 1))), "offs": striped(np.random.permutation(S)[:N])}


def reference(x, wd, y, w, b, offs):
    idx = offs[:16].T.reshape(-1)
    z = f64(wd).T @ f64(x)
    z[:, idx] += f64(w).T @ f64(y)
    return gelu_tanh(z + f64(b))

@@ -1,0 +1,60 @@
+import concourse.mybir as mybir
+
+BF16, F32, U16 = mybir.dt.bfloat16, mybir.dt.float32, mybir.dt.uint16
+GELU_TANH = mybir.ActivationFunctionType.Gelu_apprx_tanh
+
+P = 128
+S, A, K, M, N = 512, 128, 256, 512, 128
+FLOPS = 2 * A * S * M + 2 * K * N * M
+
+
+def tile_rows_fillproj_gelu_kernel(tc, x, wd, y, w, b, offs, out):
+    nc = tc.nc
+    blocks = M // P
+    depth = K // P
+    with (
+        tc.tile_pool(name="held", bufs=1) as held,
+        tc.psum_pool(name="psum", bufs=1) as psum,
+    ):
+        x_tile = held.tile([P, S], BF16, name="x_tile")
+        wd_tile = held.tile([P, M], BF16, name="wd_tile")
+        offsets = held.tile([P, N // 16], U16, name="offsets")
+        y_tile = held.tile([P, depth, N], BF16, name="y_tile")
+        w_tile = held.tile([P, depth, M], BF16, name="w_tile")
+        b_tile = held.tile([P, blocks], F32, name="b_tile")
+
+        nc.sync.dma_start(x_tile[:], x)
+        nc.sync.dma_start(wd_tile[:], wd)
+        nc.sync.dma_start(offsets[:], offs)
+        nc.sync.dma_start(y_tile[:], y.rearrange("(p k) n -> p k n", k=depth))
+        nc.sync.dma_start(w_tile[:], w.rearrange("(p k) m -> p k m", k=depth))
+        nc.sync.dma_start(b_tile[:], b.rearrange("(a p) o -> p (a o)", p=P))
+
+        zeros = held.tile([P, S], BF16, name="zeros")
+        nc.vector.memset(zeros[:], 0.0)
+        spare = psum.tile([P, S], F32, name="spare")
+        for i in range(5):
+            nc.tensor.matmul(spare[:], zeros[:, 0:P], zeros[:], start=True, stop=True)
+        one = held.tile([P, 1], F32, name="one")
+        nc.vector.memset(one[:], 0.0)
+        early = held.tile([P, 1], F32, name="early")
+        nc.scalar.activation(early[:], one[:], GELU_TANH)
+
+        windows = [psum.tile([P, S], F32, name=f"window{a}") for a in range(blocks)]
+        for a in range(blocks):
+            nc.tensor.matmul(windows[a][:], wd_tile[:, a * P:(a + 1) * P], x_tile[:], start=True, stop=False)
+
+        for a in range(blocks):
+            for k in range(depth):
+                nc.tensor.matmul(
+                    windows[a][:].indirect(offsets[:]),
+                    w_tile[:, k, a * P:(a + 1) * P],
+                    y_tile[:, k, :],
+                    start=False,
+                    stop=(k == depth - 1),
+                )
+
+        for a in range(blocks):
+            result = held.tile([P, S], F32, name=f"result{a}")
+            nc.scalar.activation(result[:], windows[a][:], GELU_TANH, bias=b_tile[:, a:a + 1])
+            nc.sync.dma_start(out[a * P:(a + 1) * P, :], result[:])

@@ -28,7 +28,7 @@ def tile_rows_fillproj_gelu_kernel(tc, x, wd, y, w, b, offs, out):
         nc.sync.dma_start(offsets[:], offs)
         nc.sync.dma_start(y_tile[:], y.rearrange("(p k) n -> p k n", k=depth))
         nc.sync.dma_start(w_tile[:], w.rearrange("(p k) m -> p k m", k=depth))
-        nc.sync.dma_start(b_tile[:], b.rearrange("(a p) o -> p (a o)", p=P))
+        nc.sync.dma_start(b_tile[:], b.rearrange("(p a) o -> p (a o)", p=P))
 
         zeros = held.tile([P, S], BF16, name="zeros")
         nc.vector.memset(zeros[:], 0.0)
@@ -42,19 +42,20 @@ def tile_rows_fillproj_gelu_kernel(tc, x, wd, y, w, b, offs, out):
 
         windows = [psum.tile([P, S], F32, name=f"window{a}") for a in range(blocks)]
         for a in range(blocks):
-            nc.tensor.matmul(windows[a][:], wd_tile[:, a * P:(a + 1) * P], x_tile[:], start=True, stop=False)
+            nc.tensor.matmul(windows[a][:], wd_tile[:, a::blocks], x_tile[:], start=True, stop=False)
 
         for a in range(blocks):
             for k in range(depth):
                 nc.tensor.matmul(
                     windows[a][:].indirect(offsets[:]),
-                    w_tile[:, k, a * P:(a + 1) * P],
+                    w_tile[:, k, a::blocks],
                     y_tile[:, k, :],
                     start=False,
                     stop=(k == depth - 1),
                 )
 
+        out_rows = out.rearrange("(p a) s -> p a s", a=blocks)
         for a in range(blocks):
             result = held.tile([P, S], F32, name=f"result{a}")
             nc.scalar.activation(result[:], windows[a][:], GELU_TANH, bias=b_tile[:, a:a + 1])
-            nc.sync.dma_start(out[a * P:(a + 1) * P, :], result[:])
+            nc.sync.dma_start(out_rows[:, a, :], result[:])

@@ -30,10 +30,10 @@ def tile_rows_fillproj_gelu_kernel(tc, x, wd, y, w, b, offs, out):
         nc.sync.dma_start(w_tile[:], w.rearrange("(p k) m -> p k m", k=depth))
         nc.sync.dma_start(b_tile[:], b.rearrange("(p a) o -> p (a o)", p=P))
 
-        zeros = held.tile([P, S], BF16, name="zeros")
+        zeros = held.tile([P, S // 2], BF16, name="zeros")
         nc.vector.memset(zeros[:], 0.0)
-        spare = psum.tile([P, S], F32, name="spare")
-        for i in range(5):
+        spare = psum.tile([P, S // 2], F32, name="spare")
+        for i in range(6):
             nc.tensor.matmul(spare[:], zeros[:, 0:P], zeros[:], start=True, stop=True)
         one = held.tile([P, 1], F32, name="one")
         nc.vector.memset(one[:], 0.0)

@@ -55,7 +55,11 @@ def tile_rows_fillproj_gelu_kernel(tc, x, wd, y, w, b, offs, out):
                 )
 
         out_rows = out.rearrange("(p a) s -> p a s", a=blocks)
+        half = S // 2
         for a in range(blocks):
             result = held.tile([P, S], F32, name=f"result{a}")
-            nc.scalar.activation(result[:], windows[a][:], GELU_TANH, bias=b_tile[:, a:a + 1])
-            nc.sync.dma_start(out_rows[:, a, :], result[:])
+            for c in range(0, S, half):
+                nc.scalar.activation(
+                    result[:, c:c + half], windows[a][:, c:c + half], GELU_TANH, bias=b_tile[:, a:a + 1]
+                )
+                nc.sync.dma_start(out_rows[:, a, c:c + half], result[:, c:c + half])

import concourse.mybir as mybir

BF16, F32, U16 = mybir.dt.bfloat16, mybir.dt.float32, mybir.dt.uint16
GELU_TANH = mybir.ActivationFunctionType.Gelu_apprx_tanh

P = 128
S, A, K, M, N = 512, 128, 256, 512, 128
FLOPS = 2 * A * S * M + 2 * K * N * M


def tile_rows_fillproj_gelu_kernel(tc, x, wd, y, w, b, offs, out):
    nc = tc.nc
    blocks = M // P
    depth = K // P
    with (
        tc.tile_pool(name="held", bufs=1) as held,
        tc.psum_pool(name="psum", bufs=1) as psum,
    ):
        x_tile = held.tile([P, S], BF16, name="x_tile")
        wd_tile = held.tile([P, M], BF16, name="wd_tile")
        offsets = held.tile([P, N // 16], U16, name="offsets")
        y_tile = held.tile([P, depth, N], BF16, name="y_tile")
        w_tile = held.tile([P, depth, M], BF16, name="w_tile")
        b_tile = held.tile([P, blocks], F32, name="b_tile")

        nc.sync.dma_start(x_tile[:], x)
        nc.sync.dma_start(wd_tile[:], wd)
        nc.sync.dma_start(offsets[:], offs)
        nc.sync.dma_start(y_tile[:], y.rearrange("(p k) n -> p k n", k=depth))
        nc.sync.dma_start(w_tile[:], w.rearrange("(p k) m -> p k m", k=depth))
        nc.sync.dma_start(b_tile[:], b.rearrange("(p a) o -> p (a o)", p=P))

        zeros = held.tile([P, S // 2], BF16, name="zeros")
        nc.vector.memset(zeros[:], 0.0)
        spare = psum.tile([P, S // 2], F32, name="spare")
        for i in range(6):
            nc.tensor.matmul(spare[:], zeros[:, 0:P], zeros[:], start=True, stop=True)
        one = held.tile([P, 1], F32, name="one")
        nc.vector.memset(one[:], 0.0)
        early = held.tile([P, 1], F32, name="early")
        nc.scalar.activation(early[:], one[:], GELU_TANH)

        windows = [psum.tile([P, S], F32, name=f"window{a}") for a in range(blocks)]
        for a in range(blocks):
            nc.tensor.matmul(windows[a][:], wd_tile[:, a::blocks], x_tile[:], start=True, stop=False)

        for a in range(blocks):
            for k in range(depth):
                nc.tensor.matmul(
                    windows[a][:].indirect(offsets[:]),
                    w_tile[:, k, a::blocks],
                    y_tile[:, k, :],
                    start=False,
                    stop=(k == depth - 1),
                )

        out_rows = out.rearrange("(p a) s -> p a s", a=blocks)
        half = S // 2
        for a in range(blocks):
            result = held.tile([P, S], F32, name=f"result{a}")
            for c in range(0, S, half):
                nc.scalar.activation(
                    result[:, c:c + half], windows[a][:, c:c + half], GELU_TANH, bias=b_tile[:, a:a + 1]
                )
                nc.sync.dma_start(out_rows[:, a, c:c + half], result[:, c:c + half])
